import numpy as np
import ml_dtypes


def mxq(x, axis, fmt="e4m3"):
    dtype, down = {"e4m3": (ml_dtypes.float8_e4m3fn, 7), "e5m2": (ml_dtypes.float8_e5m2, 14)}[fmt]
    v = np.moveaxis(np.asarray(x, np.float32).astype(ml_dtypes.bfloat16).astype(np.float64), axis, -1)
    blocks = v.reshape(v.shape[:-1] + (-1, 32))
    amax = np.abs(blocks).max(-1, keepdims=True)
    byte = np.maximum(np.where(amax > 0, np.frexp(amax)[1] - 1 + 127, 0) - down, 1)
    scale = np.exp2(byte - 127.0)
    codes = (blocks / scale).astype(np.float32).astype(dtype).astype(np.float64)
    return np.moveaxis((codes * scale).reshape(v.shape), -1, axis)


WIDE = False


def mx_kscale(k):
    if not WIDE:
        return np.ones(k)
    levels = np.array([10, -10, 5, -5, 0])
    if k % 512:
        return np.exp2(np.random.permutation(np.resize(levels, k // 32))).repeat(32)
    a = np.empty((k // 512, 16))
    for p in range(k // 512):
        a[p, :8] = np.random.permutation(np.resize(levels, 8))
        for g in range(8):
            far = levels[np.abs(levels - a[p, g]) >= 10]
            a[p, g + 8] = far[np.random.randint(len(far))]
    return np.exp2(a.ravel()).repeat(32)


def f64(x):
    return np.asarray(x).astype(np.float64)


def striped8(idx):
    return np.concatenate([v.reshape(-1, 16).T for v in idx]).astype(np.uint16)


def unstriped8(offs):
    return np.stack([offs[16 * g:16 * g + 16].T.reshape(-1) for g in range(8)]).astype(np.int64)


E2M1 = np.array([0.0, 0.5, 1.0, 1.5, 2.0, 3.0, 4.0, 6.0, -0.0, -0.5, -1.0, -1.5, -2.0, -3.0, -4.0, -6.0])


def pack_weight(w, fmt):
    k, n = w.shape
    w = f64(np.asarray(w, np.float32).astype(ml_dtypes.bfloat16)).reshape(k // 32, 32, n)
    amax = np.abs(w).max(1)
    if fmt == "e4m3":
        byte = np.frexp(amax)[1] - 1 + 127 - 7
    else:
        mant, ex = np.frexp(amax / 6.0)
        byte = np.where(mant > 0.5, ex, ex - 1) + 127
    byte = np.clip(np.where(amax > 0, byte, 1), 1, 254)
    scaled = (w * np.exp2(127.0 - byte)[:, None, :]).reshape(k, n).astype(np.float32)
    by_word = np.ascontiguousarray(scaled.reshape(k // 512, 128, 4, n).transpose(0, 1, 3, 2))
    if fmt == "e4m3":
        words = by_word.astype(ml_dtypes.float8_e4m3fn).view(np.uint8)
    else:
        c = by_word.astype(ml_dtypes.float4_e2m1fn).view(np.uint8) & 0xF
        words = (c[..., 0::2] | (c[..., 1::2] << 4)).reshape(k // 512, 128, 2 * n)
    return np.ascontiguousarray(words), np.ascontiguousarray(byte.astype(np.uint8).reshape(k // 512, 16, n))


def unpack_weight(words, scales, fmt):
    g, _, n = scales.shape
    words = np.ascontiguousarray(words).reshape(g, 128, n, -1)
    if fmt == "e4m3":
        vals = words.view(ml_dtypes.float8_e4m3fn).astype(np.float64)
    else:
        nib = np.empty((g, 128, n, 4), np.uint8)
        nib[..., 0::2] = words & 0xF
        nib[..., 1::2] = words >> 4
        vals = E2M1[nib]
    vals = vals * np.repeat(np.exp2(scales.astype(np.float64) - 127.0), 8, axis=1)[..., None]
    return vals.transpose(0, 1, 3, 2).reshape(g * 512, n)


def gelu(v):
    return 0.5 * v * (1.0 + np.tanh(np.sqrt(2.0 / np.pi) * (v + 0.044715 * v**3)))


K, M, T, S = 1024, 512, 4096, 2048


def setup_inputs():
    n = np.random.standard_normal
    s = mx_kscale(K)[:, None]
    s2 = mx_kscale(512)[:, None]
    p_w4 = pack_weight(n((K, M)) / np.sqrt(K) / s, "e2m1")
    return {
        "x": (n((K, S)) * s).astype(np.float32),
        "w4_words": p_w4[0],
        "w4_scales": p_w4[1],
        "c": (n((512, S)) * s2).astype(np.float32),
        "u": (n((512, M)) / np.sqrt(512) / s2).astype(np.float32),
        "b": (0.3 * n(512)).astype(np.float32),
        "wgo": np.repeat(np.random.uniform(0.5, 2.0, (8, S)), 16, axis=0).astype(np.float32),
        "offs": striped8(np.stack([np.random.permutation(T)[:S] for _ in range(8)])),
    }


def reference(x, w4_words, w4_scales, c, u, b, wgo, offs):
    x_ = mxq(f64(x), 0, "e4m3")
    w4_ = unpack_weight(w4_words, w4_scales, "e2m1")
    c_ = mxq(f64(c), 0, "e4m3")
    u_ = mxq(f64(u), 0, "e4m3")
    y = w4_.T @ x_ + u_.T @ c_
    place = unstriped8(offs)[np.arange(M) % 128 // 16]
    out = np.zeros((M, T))
    out[np.arange(M)[:, None], place] = f64(wgo)[np.arange(M) % 128] * (gelu(y + f64(b)[:, None]))
    return out

from contextlib import ExitStack

import concourse.mybir as mybir

K, M, T, S, L = 1024, 512, 4096, 2048, 512
FLOPS = 2 * (K + L) * M * S

F32 = mybir.dt.float32
BF16 = mybir.dt.bfloat16
I32 = mybir.dt.int32
U32 = mybir.dt.uint32
U16 = mybir.dt.uint16
U8 = mybir.dt.uint8
FP8X4 = mybir.dt.float8_e4m3fn_x4
FP4X4 = mybir.dt.float4_e2m1fn_x4
GELU = mybir.ActivationFunctionType.Gelu_apprx_tanh
MULT = mybir.AluOpType.mult

P = 128
PACK = 4
K_PASS = P * PACK
BANK = 512
LANES = 16
CHUNKS = (256, 256, 256, 256, 512, 512)
PAGES = 3


def interleave_views(grouped, raw):
    dst = grouped.rearrange("p (c i t) -> p c t i", i=4, t=PACK)
    src = raw.rearrange("p (t c i) -> p c t i", t=PACK, i=4)
    return dst, src


def tile_list_hscat_d_gelu_kernel(tc, x, w4_words, w4_scales, c, u, b, wgo, offs, out):
    nc = tc.nc
    starts = [sum(CHUNKS[:j]) for j in range(len(CHUNKS))]
    sources = (x[0:K_PASS, :], x[K_PASS:K, :], c)

    with ExitStack() as ctx:
        keep = ctx.enter_context(tc.tile_pool(name="keep", bufs=1))
        stage = ctx.enter_context(tc.tile_pool(name="stage", bufs=4))
        psum = ctx.enter_context(tc.psum_pool(name="psum", bufs=8))

        offsets = keep.tile([P, S // LANES], U16, name="offsets")
        w_parts = ((0, 128), (128, 512))
        w_words = [keep.tile([P, 2 * 2 * (n1 - n0)], U8, name=f"w_words{n0}", align_bytes=64) for n0, n1 in w_parts]
        w_scales = keep.tile([P, 2 * M], U8, name="w_scales", align_bytes=64)
        bias = keep.tile([P, M // P], F32, name="bias")
        gains = keep.tile([P, S], F32, name="gains")
        u_codes = keep.tile([P, M], U32, name="u_codes", align_bytes=64)
        u_scales = keep.tile([P, M], U8, name="u_scales", align_bytes=64)
        codes = [keep.tile([P, S], U32, name=f"codes{a}", align_bytes=64) for a in range(3)]
        scales = [keep.tile([P, S], U8, name=f"scales{a}", align_bytes=64) for a in range(3)]
        pages = [keep.tile([P, T], F32, name=f"page{m}") for m in range(PAGES - 1)]
        opening = keep.tile([P, PACK * (CHUNKS[0] + P)], BF16, name="opening", tag="late_page", align_bytes=64)
        raw = [[keep.tile([P, PACK * w], F32, name=f"raw{j}_{a}") for a in range(3)] for j, w in enumerate(CHUNKS)]
        u_parts = ((0, 128), (128, 384), (384, 512))
        u_raw = [keep.tile([P, PACK * (n1 - n0)], F32, name=f"u_raw{n0}") for n0, n1 in u_parts]
        first = keep.tile([P, 2 * CHUNKS[0]], F32, name="first")
        last = keep.tile([P, S], F32, name="last")

        def load_rows(tile, rows):
            nc.sync.dma_start(tile[:].rearrange("p (t w) -> p t w", t=PACK), rows.rearrange("(p t) w -> p t w", t=PACK))

        def load_piece(j, a):
            load_rows(raw[j][a], sources[a][:, starts[j] : starts[j] + CHUNKS[j]])

        def load_u(i):
            load_rows(u_raw[i], u[:, u_parts[i][0] : u_parts[i][1]])

        def load_gains(j):
            cols = slice(starts[j], starts[j] + CHUNKS[j])
            nc.sync.dma_start(gains[:, cols], wgo[:, cols])

        def load_w(i):
            n0, n1 = w_parts[i]
            nc.sync.dma_start(
                w_words[i][:].bitcast(I32).rearrange("p (a n) -> p a n", a=2),
                w4_words[:, :, 2 * n0 : 2 * n1].bitcast(I32).rearrange("a p n -> p a n"),
            )

        def w_tile(a, m):
            i = min(m, 1)
            n0, n1 = w_parts[i]
            at = 2 * (a * (n1 - n0) + m * P - n0)
            return w_words[i][:, at : at + 2 * P].bitcast(FP4X4)

        def quantise(tile, out_codes, out_scales, on_vector=False, grouped=None):
            if grouped is None:
                grouped = stage.tile([P, tile.shape[1]], BF16, name="grouped", align_bytes=64)[:]
            dst, src = interleave_views(grouped, tile[:])
            if on_vector:
                nc.vector.tensor_copy(dst, src)
            else:
                nc.scalar.copy(dst, src)
            nc.vector.quantize_mx(out=out_codes.bitcast(FP8X4), scales=out_scales, in_=grouped)

        def quantise_piece(j, a, grouped=None):
            cols = slice(starts[j], starts[j] + CHUNKS[j])
            quantise(raw[j][a], codes[a][:, cols], scales[a][:, cols], False, grouped)

        def quantise_u(i, on_vector=False, grouped=None):
            cols = slice(u_parts[i][0], u_parts[i][1])
            quantise(u_raw[i], u_codes[:, cols], u_scales[:, cols], on_vector, grouped)

        def multiply(m, j0, width):
            acc = psum.tile([P, width], F32, name="acc")
            step = width if width == BANK else P
            for a in range(2):
                for n0 in range(0, width, step):
                    cols = slice(j0 + n0, j0 + n0 + step)
                    nc.tensor.matmul_mx(
                        out=acc[:, n0 : n0 + step],
                        lhsT=w_tile(a, m),
                        lhsT_scale=w_scales[:, a * M + m * P : a * M + (m + 1) * P],
                        rhs=codes[a][:, cols].bitcast(FP8X4),
                        rhs_scale=scales[a][:, cols],
                        start=(a == 0 and n0 == 0),
                        stop=False,
                    )
            cols = slice(j0, j0 + width)
            nc.tensor.matmul_mx(
                out=acc[:],
                lhsT=u_codes[:, m * P : (m + 1) * P].bitcast(FP8X4),
                lhsT_scale=u_scales[:, m * P : (m + 1) * P],
                rhs=codes[2][:, cols].bitcast(FP8X4),
                rhs_scale=scales[2][:, cols],
                start=False,
                stop=True,
            )
            return acc

        def activate(m, acc, values):
            nc.scalar.activation(values, acc[:], GELU, bias=bias[:, m : m + 1])

        def scatter(page, values, j0, width):
            window = page[:].indirect(offsets[:, j0 // LANES : (j0 + width) // LANES])
            nc.vector.tensor_tensor(window, values, gains[:, j0 : j0 + width], MULT)

        load_piece(0, 0)
        for q in range(4):
            nc.sync.dma_start(
                w_scales[32 * q : 32 * q + 4, :].bitcast(I32).rearrange("r (a n) -> r a n", a=2),
                w4_scales.bitcast(I32)[:, 4 * q : 4 * q + 4, :].rearrange("a r n -> r a n"),
            )
        load_w(0)
        load_piece(0, 1)
        load_piece(0, 2)
        load_u(0)
        with nc.allow_non_contiguous_dma(reason="one bias value for each partition and row tile"):
            nc.sync.dma_start(bias[:], b.rearrange("(m p) -> p m", p=P))
        nc.sync.dma_start(offsets[:], offs)
        load_gains(0)
        load_w(1)
        load_u(1)
        for j in range(1, len(CHUNKS)):
            for a in range(3):
                load_piece(j, a)
            load_gains(j)
        load_u(2)

        nc.vector.memset(pages[0][:, 0 : T // 2 - 1], 0.0)
        nc.vector.memset(pages[0][:, T // 2 - 1 : T], 0.0)
        nc.gpsimd.memset(pages[1][:], 0.0)
        quantise_piece(0, 0)
        quantise_piece(0, 1)
        quantise_piece(0, 2, opening[:, 0 : PACK * CHUNKS[0]])
        quantise_u(0, True, opening[:, PACK * CHUNKS[0] :])
        pages.append(keep.tile([P, T], F32, name="late_page", tag="late_page", align_bytes=64))
        for t0 in range(0, T, 512):
            nc.gpsimd.memset(pages[2][:, t0 : t0 + 512], 0.0)

        for j, width in enumerate(CHUNKS):
            final = j == len(CHUNKS) - 1
            for m in range(PAGES):
                if not final:
                    quantise_piece(j + 1, m)
                if j == 0 and m < 2:
                    values = first[:, m * width : (m + 1) * width]
                elif final:
                    values = raw[j][m][:, width : 2 * width]
                else:
                    values = raw[j + 1][m][:, 0:width]
                activate(m, multiply(m, starts[j], width), values)
                scatter(pages[m], values, starts[j], width)
                if j == 0 and m == 0:
                    quantise_u(1)
                if final:
                    nc.sync.dma_start(out[m * P : (m + 1) * P, :], pages[m][:])

        quantise_u(2)
        m = PAGES
        for j0 in range(0, S, BANK):
            activate(m, multiply(m, j0, BANK), last[:, j0 : j0 + BANK])
        scatter(pages[0], last[:], 0, S)
        nc.sync.dma_start(out[m * P : (m + 1) * P, :], pages[0][:])
